import numpy as np
import ml_dtypes


def mxq(x, axis, fmt="e4m3"):
    dtype, down = {"e4m3": (ml_dtypes.float8_e4m3fn, 7), "e5m2": (ml_dtypes.float8_e5m2, 14)}[fmt]
    v = np.moveaxis(np.asarray(x, np.float32).astype(ml_dtypes.bfloat16).astype(np.float64), axis, -1)
    blocks = v.reshape(v.shape[:-1] + (-1, 32))
    amax = np.abs(blocks).max(-1, keepdims=True)
    byte = np.maximum(np.where(amax > 0, np.frexp(amax)[1] - 1 + 127, 0) - down, 1)
    scale = np.exp2(byte - 127.0)
    codes = (blocks / scale).astype(np.float32).astype(dtype).astype(np.float64)
    return np.moveaxis((codes * scale).reshape(v.shape), -1, axis)


WIDE = False


def mx_kscale(k):
    if not WIDE:
        return np.ones(k)
    levels = np.array([10, -10, 5, -5, 0])
    if k % 512:
        return np.exp2(np.random.permutation(np.resize(levels, k // 32))).repeat(32)
    a = np.empty((k // 512, 16))
    for p in range(k // 512):
        a[p, :8] = np.random.permutation(np.resize(levels, 8))
        for g in range(8):
            far = levels[np.abs(levels - a[p, g]) >= 10]
            a[p, g + 8] = far[np.random.randint(len(far))]
    return np.exp2(a.ravel()).repeat(32)


def f64(x):
    return np.asarray(x).astype(np.float64)


def striped(idx):
    return np.tile(idx.reshape(-1, 16).T, (8, 1)).astype(np.uint16)


def unstriped(offs):
    return offs[:16].T.reshape(-1).astype(np.int64)


def pack_weight(w):
    k, n = w.shape
    w = f64(np.asarray(w, np.float32).astype(ml_dtypes.bfloat16)).reshape(k // 32, 32, n)
    amax = np.abs(w).max(1)
    byte = np.clip(np.where(amax > 0, np.frexp(amax)[1] - 1 + 127 - 7, 1), 1, 254)
    scaled = (w * np.exp2(127.0 - byte)[:, None, :]).reshape(k, n).astype(np.float32)
    words = np.ascontiguousarray(scaled.reshape(k // 512, 128, 4, n).transpose(0, 1, 3, 2)).astype(ml_dtypes.float8_e4m3fn).view(np.uint8)
    return words, np.ascontiguousarray(byte.astype(np.uint8).reshape(k // 512, 16, n))


def unpack_weight(words, scales):
    g, p, n, _ = words.shape
    vals = np.ascontiguousarray(words).view(ml_dtypes.float8_e4m3fn).astype(np.float64) * np.repeat(np.exp2(scales.astype(np.float64) - 127.0), 8, axis=1)[..., None]
    return vals.transpose(0, 1, 3, 2).reshape(g * 512, n)


K, T, S, N = 1024, 1024, 512, 128
P = 2 ** 7


def setup_inputs():
    n = np.random.standard_normal
    s = mx_kscale(K)[:, None]
    packed_xT = pack_weight(n((K, T)) * s)
    return {
        "x_words": packed_xT[0],
        "x_scales": packed_xT[1],
        "w1": (n((K, N)) / np.sqrt(K) / s).astype(np.float32),
        "mx": (n((N, S)) / np.sqrt(3)).astype(np.float32),
        "my": (n((N, S)) / np.sqrt(3)).astype(np.float32),
        "mz": (n((N, S)) / np.sqrt(3)).astype(np.float32),
        "exch": (np.tile(np.random.uniform(0.3, 1.0, S), (P, 1))).astype(np.float32),
        "offs": striped(np.random.permutation(T)[:S]),
        "pos1": striped(np.random.permutation(S)[:S]),
        "pos2": striped(np.random.permutation(S)[:S]),
    }


def reference(x_words, x_scales, w1, mx, my, mz, exch, offs, pos1, pos2):
    hz = (f64(mz)[:, unstriped(pos1)] + f64(mz)[:, unstriped(pos2)]) * f64(exch)[:1] + 0.3 * f64(mz)
    hy = (f64(my)[:, unstriped(pos1)] + f64(my)[:, unstriped(pos2)]) * f64(exch)[:1] + 0.3 * f64(my)
    tox = f64(my) * hz - (f64(mz) * hy)
    xq = unpack_weight(x_words, x_scales)[:, unstriped(offs)]
    y = mxq(f64(w1), 0, "e4m3").T @ xq
    hx = (f64(mx)[:, unstriped(pos1)] + f64(mx)[:, unstriped(pos2)]) * f64(exch)[:1] + y
    toy = f64(mz) * hx - (f64(mx) * hz)
    toz = f64(mx) * hy - (f64(my) * hx)
    return np.sqrt((tox) ** 2 + (toy) ** 2 + (toz) ** 2 + 0.02)

@@ -1,0 +1,233 @@
+from contextlib import ExitStack
+
+import concourse.mybir as mybir
+from concourse.masks import make_identity
+
+K, T, S, N = 1024, 1024, 512, 128
+FLOPS = 2 * K * S * N
+
+F32 = mybir.dt.float32
+BF16 = mybir.dt.bfloat16
+I32 = mybir.dt.int32
+U32 = mybir.dt.uint32
+U16 = mybir.dt.uint16
+U8 = mybir.dt.uint8
+FP8X4 = mybir.dt.float8_e4m3fn_x4
+ACT = mybir.ActivationFunctionType
+ALU = mybir.AluOpType
+
+P = 128
+PASSES = 2
+HALF = S // 2
+BLK = 128
+
+
+def tile_picked_yllg_torq_p_kernel(tc, x_words, x_scales, w1, mx, my, mz, exch, offs, pos1, pos2, out):
+    nc = tc.nc
+    with ExitStack() as ctx:
+        lists = ctx.enter_context(tc.tile_pool(name="lists", bufs=1))
+        sb = ctx.enter_context(tc.tile_pool(name="sb", bufs=1))
+        ps = ctx.enter_context(tc.psum_pool(name="ps", bufs=1))
+
+        def cols(h):
+            return slice(h * HALF, (h + 1) * HALF)
+
+        def entries(h):
+            return slice(h * HALF // 16, (h + 1) * HALF // 16)
+
+        def turn(dst, src, start, stop):
+            nc.tensor.matmul(dst, lhsT=src, rhs=ident[:], start=start, stop=stop, is_transpose=True)
+
+        offs_t = lists.tile([P, S // 16], U16, name="offs_t")
+        pos1_t = lists.tile([P, S // 16], U16, name="pos1_t")
+        pos2_t = lists.tile([P, S // 16], U16, name="pos2_t")
+
+        scale_win = sb.tile([P, T], U8, name="scale_win", align_bytes=64)
+        nc.vector.memset(scale_win[:].bitcast(I32), 0)
+
+        def f32(name, shape, tag=None):
+            return sb.tile([P] + shape, F32, name=name, tag=tag or name, align_bytes=64)
+
+        mx_t = f32("mx_t", [S])
+        my_t = f32("my_t", [S])
+        mz_t = f32("mz_t", [S])
+        e_col = f32("e_col", [4])
+        word_win = [sb.tile([P, T], U32, name=f"word_win{g}", tag=f"win{g}", align_bytes=64) for g in range(PASSES)]
+        w_raw = f32("w_raw", [PASSES, 4, N])
+
+        def load_words(g):
+            nc.sync.dma_start(out=word_win[g][:].bitcast(I32), in_=x_words[g].rearrange("p n t -> p (n t)").bitcast(I32))
+
+        nc.sync.dma_start(pos1_t[:], pos1)
+        nc.sync.dma_start(out=my_t[:], in_=my)
+        nc.sync.dma_start(pos2_t[:], pos2)
+        with nc.allow_non_contiguous_dma(reason="one exchange constant a partition"):
+            nc.sync.dma_start(out=e_col[:], in_=exch[0:1, :].rearrange("o (b p) -> p (o b)", p=P))
+        nc.sync.dma_start(out=mx_t[:], in_=mx)
+        nc.sync.dma_start(offs_t[:], offs)
+        load_words(0)
+        for q in range(4):
+            nc.sync.dma_start(out=scale_win[32 * q : 32 * q + 8, :].bitcast(I32), in_=x_scales[:, 4 * q : 4 * q + 4, :].bitcast(I32))
+        nc.sync.dma_start(out=w_raw[:], in_=w1.rearrange("(g p j) n -> p g j n", g=PASSES, j=4))
+        nc.sync.dma_start(out=mz_t[:], in_=mz)
+        load_words(1)
+
+        ident = f32("ident", [P])
+        make_identity(nc, ident[:])
+
+        def picked(win, lst, lo, hi):
+            return win[:].indirect(lst[:, lo // 16 : hi // 16])
+
+        def fetch_pair(name, win, h, tag=None):
+            pair = f32(name, [2, HALF], tag)
+            for c, lst in enumerate((pos1_t, pos2_t)):
+                nc.scalar.activation(out=pair[:, c, :], in_=picked(win, lst, h * HALF, (h + 1) * HALF), func=ACT.Copy)
+            return pair
+
+        def add(dst, a, b):
+            nc.vector.tensor_tensor(out=dst, in0=a, in1=b, op=ALU.add)
+
+        def mul(dst, a, b):
+            nc.vector.tensor_tensor(out=dst, in0=a, in1=b, op=ALU.mult)
+
+        def flat(bank):
+            return bank[:].rearrange("p b n -> p (b n)")
+
+        e_bank = ps.tile([P, 4, BLK], F32, name="e_bank")
+        for b in range(4):
+            nc.tensor.transpose(e_bank[:, b, :], e_col[:, b : b + 1].to_broadcast([P, BLK]), ident[:])
+
+        gy = f32("gy", [S])
+        by1 = f32("by1", [HALF])
+        aby = fetch_pair("aby", my_t, 0)
+        for b in range(2):
+            lo = HALF + b * BLK
+            nc.vector.tensor_copy(out=by1[:, b * BLK : (b + 1) * BLK], in_=picked(my_t, pos1_t, lo, lo + BLK))
+        for b in range(2):
+            lo = HALF + b * BLK
+            add(gy[:, lo : lo + BLK], picked(my_t, pos2_t, lo, lo + BLK), by1[:, b * BLK : (b + 1) * BLK])
+        add(gy[:, cols(0)], aby[:, 0, :], aby[:, 1, :])
+        nex = f32("nex", [S])
+        nc.vector.scalar_tensor_tensor(out=nex[:], in0=mx_t[:], scalar=-1.0, in1=flat(e_bank), op0=ALU.mult, op1=ALU.mult)
+        abx = [fetch_pair(f"abx{h}", mx_t, h) for h in range(2)]
+
+        words = [sb.tile([P, S], U32, name=f"words{g}", align_bytes=64) for g in range(PASSES)]
+        nc.vector.tensor_copy(out=words[0][:], in_=word_win[0][:].indirect(offs_t[:]))
+        scales = sb.tile([P, S], U8, name="scales", align_bytes=64)
+        nc.vector.tensor_copy(out=scales[:], in_=scale_win[:].indirect(offs_t[:]))
+
+        gx_bank = [ps.tile([P, 2, BLK], F32, name=f"gx_bank{h}", tag=f"out{h}") for h in range(2)]
+        ex_bank = [ps.tile([P, 2, BLK], F32, name=f"ex_bank{h}") for h in range(2)]
+
+        def sum_x(h):
+            for c in range(2):
+                for b in range(2):
+                    turn(gx_bank[h][:, b, :], abx[h][:, c, b * BLK : (b + 1) * BLK], start=(c == 0 and b == 0), stop=(c == 1 and b == 1))
+
+        def exchange_x(h, tag):
+            ex_t = f32(f"ex_t{h}", [2, BLK], tag)
+            for b in range(2):
+                nc.scalar.activation(out=ex_t[:, b, :], in_=gx_bank[h][:, b, :], func=ACT.Copy, scale=e_col[:, 2 * h + b : 2 * h + b + 1])
+            for b in range(2):
+                turn(ex_bank[h][:, b, :], ex_t[:, b, :], start=(b == 0), stop=False)
+
+        sum_x(0)
+        sum_x(1)
+        exchange_x(0, None)
+        w_bf = sb.tile([P, PASSES, N, 4], BF16, name="w_bf", align_bytes=64)
+        nc.scalar.copy(out=w_bf[:].rearrange("p g (c i) j -> p g c j i", i=4), in_=w_raw[:].rearrange("p g j (c i) -> p g c j i", i=4))
+        exchange_x(1, "w_raw")
+        abz = [fetch_pair(f"abz{h}", mz_t, h) for h in range(2)]
+
+        px = f32("px", [2, S])
+        nc.vector.scalar_tensor_tensor(out=px[:, 0, :], in0=gy[:], scalar=-1.0, in1=mz_t[:], op0=ALU.mult, op1=ALU.mult)
+        w_codes = sb.tile([P, PASSES * N], U32, name="w_codes", align_bytes=64)
+        w_scales = sb.tile([P, PASSES * N], U8, name="w_scales", align_bytes=64)
+        nc.vector.quantize_mx(out=w_codes[:].bitcast(FP8X4), scales=w_scales[:], in_=w_bf[:].rearrange("p g n j -> p (g n j)"))
+        for h in range(2):
+            nc.vector.tensor_copy(out=words[1][:, cols(h)], in_=word_win[1][:].indirect(offs_t[:, entries(h)]))
+
+        x_bank = ps.tile([P, 4, BLK], F32, name="x_bank", tag="e_bank")
+        for b in range(4):
+            turn(x_bank[:, b, :], px[:, 0, b * BLK : (b + 1) * BLK], start=(b == 0), stop=False)
+
+        y_bank = [ps.tile([P, 2, BLK], F32, name=f"y_bank{h}") for h in range(2)]
+        y_t = f32("y_t", [4, BLK])
+        for h in range(2):
+            for g in range(PASSES):
+                for b in range(2):
+                    j0 = h * HALF + b * BLK
+                    nc.tensor.matmul_mx(
+                        out=y_bank[h][:, b, :],
+                        lhsT=words[g][:, j0 : j0 + BLK].bitcast(FP8X4),
+                        lhsT_scale=scales[4 * g : P, j0 : j0 + BLK],
+                        rhs=w_codes[:, g * N : (g + 1) * N].bitcast(FP8X4),
+                        rhs_scale=w_scales[:, g * N : (g + 1) * N],
+                        start=(g == 0 and b == 0),
+                        stop=(g == PASSES - 1 and b == 1),
+                    )
+            nc.scalar.copy(out=y_t[:, 2 * h : 2 * h + 2, :], in_=y_bank[h][:])
+            for b in range(2):
+                turn(ex_bank[h][:, b, :], y_t[:, 2 * h + b, :], start=False, stop=(b == 1))
+
+        gz = f32("gz", [S])
+        ngz = f32("ngz", [S])
+        ngy = f32("ngy", [S], "win1")
+        hx = f32("hx", [S])
+        pyz = f32("pyz", [2, S])
+        res = f32("res", [S])
+        t_bank = [ps.tile([P, 2, BLK], F32, name=f"t_bank{c}", tag=("t_bank0", "y_bank0")[c]) for c in range(2)]
+
+        for h in range(2):
+            add(gz[:, cols(h)], abz[h][:, 0, :], abz[h][:, 1, :])
+            mul(px[:, 1, cols(h)], gz[:, cols(h)], my_t[:, cols(h)])
+            mul(ngz[:, cols(h)], nex[:, cols(h)], gz[:, cols(h)])
+        for h in range(2):
+            mul(ngy[:, cols(h)], nex[:, cols(h)], gy[:, cols(h)])
+        for b in range(4):
+            turn(x_bank[:, b, :], px[:, 1, b * BLK : (b + 1) * BLK], start=False, stop=(b == 3))
+        for c in range(2):
+            for b in range(2):
+                turn(t_bank[c][:, b, :], (ngz, ngy)[c][:, b * BLK : (b + 1) * BLK], start=(b == 0), stop=False)
+        sq_x = f32("sq_x", [4, BLK])
+        for b in range(4):
+            nc.scalar.activation(out=sq_x[:, b, :], in_=x_bank[:, b, :], func=ACT.Square, scale=e_col[:, b : b + 1])
+
+        def product(h, c):
+            mul(pyz[:, c, cols(h)], hx[:, cols(h)], (mz_t, my_t)[c][:, cols(h)])
+
+        def finish(lo, hi, total):
+            nc.scalar.activation(out=res[:, lo:hi], in_=total, func=ACT.Sqrt, bias=0.02)
+            nc.sync.dma_start(out=out[:, lo:hi], in_=res[:, lo:hi])
+
+        for h in range(2):
+            nc.vector.scalar_tensor_tensor(out=hx[:, cols(h)], in0=mx_t[:, cols(h)], scalar=-0.3, in1=flat(ex_bank[h]), op0=ALU.mult, op1=ALU.add)
+        sq_yz = f32("sq_yz", [2, 2, BLK])
+        for c in range(2):
+            product(0, c)
+            for b in range(2):
+                turn(t_bank[c][:, b, :], pyz[:, c, b * BLK : (b + 1) * BLK], start=False, stop=(b == 1))
+            nc.scalar.activation(out=sq_yz[:, c, :, :], in_=t_bank[c][:], func=ACT.Square)
+        out_bank = [ps.tile([P, 2, BLK], F32, name=f"out_bank{h}", tag=f"out{h}") for h in range(2)]
+        for h in (1, 0):
+            for b in range(2):
+                turn(out_bank[h][:, b, :], sq_x[:, 2 * h + b, :], start=(b == 0), stop=(h == 1 and b == 1))
+        for c in range(2):
+            for b in range(2):
+                turn(out_bank[0][:, b, :], sq_yz[:, c, b, :], start=False, stop=(c == 1 and b == 1))
+        product(1, 0)
+        product(1, 1)
+        tyz = f32("tyz", [2, 2, BLK])
+        sq1 = f32("sq1", [2, 2, BLK])
+        part = f32("part", [2, 2, BLK])
+        for b in range(2):
+            j0 = HALF + b * BLK
+            for c in range(2):
+                add(tyz[:, b, c, :], pyz[:, c, j0 : j0 + BLK], (ngz, ngy)[c][:, j0 : j0 + BLK])
+                nc.scalar.activation(out=sq1[:, b, c, :], in_=tyz[:, b, c, :], func=ACT.Square)
+        finish(0, HALF, flat(out_bank[0]))
+        for b in range(2):
+            add(part[:, b, 0, :], out_bank[1][:, b, :], sq1[:, b, 0, :])
+        for b in range(2):
+            add(part[:, b, 1, :], part[:, b, 0, :], sq1[:, b, 1, :])
+            finish(HALF + b * BLK, HALF + (b + 1) * BLK, part[:, b, 1, :])

@@ -44,6 +44,9 @@ def tile_picked_yllg_torq_p_kernel(tc, x_words, x_scales, w1, mx, my, mz, exch, 
 
         scale_win = sb.tile([P, T], U8, name="scale_win", align_bytes=64)
         nc.vector.memset(scale_win[:].bitcast(I32), 0)
+        warm = sb.tile([P, 2], F32, name="warm")
+        nc.vector.memset(warm[:, 0:1], 1.0)
+        nc.scalar.activation(out=warm[:, 1:2], in_=warm[:, 0:1], func=ACT.Sqrt)
 
         def f32(name, shape, tag=None):
             return sb.tile([P] + shape, F32, name=name, tag=tag or name, align_bytes=64)

from contextlib import ExitStack

import concourse.mybir as mybir
from concourse.masks import make_identity

K, T, S, N = 1024, 1024, 512, 128
FLOPS = 2 * K * S * N

F32 = mybir.dt.float32
BF16 = mybir.dt.bfloat16
I32 = mybir.dt.int32
U32 = mybir.dt.uint32
U16 = mybir.dt.uint16
U8 = mybir.dt.uint8
FP8X4 = mybir.dt.float8_e4m3fn_x4
ACT = mybir.ActivationFunctionType
ALU = mybir.AluOpType

P = 128
PASSES = 2
HALF = S // 2
BLK = 128


def tile_picked_yllg_torq_p_kernel(tc, x_words, x_scales, w1, mx, my, mz, exch, offs, pos1, pos2, out):
    nc = tc.nc
    with ExitStack() as ctx:
        lists = ctx.enter_context(tc.tile_pool(name="lists", bufs=1))
        sb = ctx.enter_context(tc.tile_pool(name="sb", bufs=1))
        ps = ctx.enter_context(tc.psum_pool(name="ps", bufs=1))

        def cols(h):
            return slice(h * HALF, (h + 1) * HALF)

        def entries(h):
            return slice(h * HALF // 16, (h + 1) * HALF // 16)

        def turn(dst, src, start, stop):
            nc.tensor.matmul(dst, lhsT=src, rhs=ident[:], start=start, stop=stop, is_transpose=True)

        offs_t = lists.tile([P, S // 16], U16, name="offs_t")
        pos1_t = lists.tile([P, S // 16], U16, name="pos1_t")
        pos2_t = lists.tile([P, S // 16], U16, name="pos2_t")

        scale_win = sb.tile([P, T], U8, name="scale_win", align_bytes=64)
        nc.vector.memset(scale_win[:].bitcast(I32), 0)
        warm = sb.tile([P, 2], F32, name="warm")
        nc.vector.memset(warm[:, 0:1], 1.0)
        nc.scalar.activation(out=warm[:, 1:2], in_=warm[:, 0:1], func=ACT.Sqrt)

        def f32(name, shape, tag=None):
            return sb.tile([P] + shape, F32, name=name, tag=tag or name, align_bytes=64)

        mx_t = f32("mx_t", [S])
        my_t = f32("my_t", [S])
        mz_t = f32("mz_t", [S])
        e_col = f32("e_col", [4])
        word_win = [sb.tile([P, T], U32, name=f"word_win{g}", tag=f"win{g}", align_bytes=64) for g in range(PASSES)]
        w_raw = f32("w_raw", [PASSES, 4, N])

        def load_words(g):
            nc.sync.dma_start(out=word_win[g][:].bitcast(I32), in_=x_words[g].rearrange("p n t -> p (n t)").bitcast(I32))

        nc.sync.dma_start(pos1_t[:], pos1)
        nc.sync.dma_start(out=my_t[:], in_=my)
        nc.sync.dma_start(pos2_t[:], pos2)
        with nc.allow_non_contiguous_dma(reason="one exchange constant a partition"):
            nc.sync.dma_start(out=e_col[:], in_=exch[0:1, :].rearrange("o (b p) -> p (o b)", p=P))
        nc.sync.dma_start(out=mx_t[:], in_=mx)
        nc.sync.dma_start(offs_t[:], offs)
        load_words(0)
        for q in range(4):
            nc.sync.dma_start(out=scale_win[32 * q : 32 * q + 8, :].bitcast(I32), in_=x_scales[:, 4 * q : 4 * q + 4, :].bitcast(I32))
        nc.sync.dma_start(out=w_raw[:], in_=w1.rearrange("(g p j) n -> p g j n", g=PASSES, j=4))
        nc.sync.dma_start(out=mz_t[:], in_=mz)
        load_words(1)

        ident = f32("ident", [P])
        make_identity(nc, ident[:])

        def picked(win, lst, lo, hi):
            return win[:].indirect(lst[:, lo // 16 : hi // 16])

        def fetch_pair(name, win, h, tag=None):
            pair = f32(name, [2, HALF], tag)
            for c, lst in enumerate((pos1_t, pos2_t)):
                nc.scalar.activation(out=pair[:, c, :], in_=picked(win, lst, h * HALF, (h + 1) * HALF), func=ACT.Copy)
            return pair

        def add(dst, a, b):
            nc.vector.tensor_tensor(out=dst, in0=a, in1=b, op=ALU.add)

        def mul(dst, a, b):
            nc.vector.tensor_tensor(out=dst, in0=a, in1=b, op=ALU.mult)

        def flat(bank):
            return bank[:].rearrange("p b n -> p (b n)")

        e_bank = ps.tile([P, 4, BLK], F32, name="e_bank")
        for b in range(4):
            nc.tensor.transpose(e_bank[:, b, :], e_col[:, b : b + 1].to_broadcast([P, BLK]), ident[:])

        gy = f32("gy", [S])
        by1 = f32("by1", [HALF])
        aby = fetch_pair("aby", my_t, 0)
        for b in range(2):
            lo = HALF + b * BLK
            nc.vector.tensor_copy(out=by1[:, b * BLK : (b + 1) * BLK], in_=picked(my_t, pos1_t, lo, lo + BLK))
        for b in range(2):
            lo = HALF + b * BLK
            add(gy[:, lo : lo + BLK], picked(my_t, pos2_t, lo, lo + BLK), by1[:, b * BLK : (b + 1) * BLK])
        add(gy[:, cols(0)], aby[:, 0, :], aby[:, 1, :])
        nex = f32("nex", [S])
        nc.vector.scalar_tensor_tensor(out=nex[:], in0=mx_t[:], scalar=-1.0, in1=flat(e_bank), op0=ALU.mult, op1=ALU.mult)
        abx = [fetch_pair(f"abx{h}", mx_t, h) for h in range(2)]

        words = [sb.tile([P, S], U32, name=f"words{g}", align_bytes=64) for g in range(PASSES)]
        nc.vector.tensor_copy(out=words[0][:], in_=word_win[0][:].indirect(offs_t[:]))
        scales = sb.tile([P, S], U8, name="scales", align_bytes=64)
        nc.vector.tensor_copy(out=scales[:], in_=scale_win[:].indirect(offs_t[:]))

        gx_bank = [ps.tile([P, 2, BLK], F32, name=f"gx_bank{h}", tag=f"out{h}") for h in range(2)]
        ex_bank = [ps.tile([P, 2, BLK], F32, name=f"ex_bank{h}") for h in range(2)]

        def sum_x(h):
            for c in range(2):
                for b in range(2):
                    turn(gx_bank[h][:, b, :], abx[h][:, c, b * BLK : (b + 1) * BLK], start=(c == 0 and b == 0), stop=(c == 1 and b == 1))

        def exchange_x(h, tag):
            ex_t = f32(f"ex_t{h}", [2, BLK], tag)
            for b in range(2):
                nc.scalar.activation(out=ex_t[:, b, :], in_=gx_bank[h][:, b, :], func=ACT.Copy, scale=e_col[:, 2 * h + b : 2 * h + b + 1])
            for b in range(2):
                turn(ex_bank[h][:, b, :], ex_t[:, b, :], start=(b == 0), stop=False)

        sum_x(0)
        sum_x(1)
        exchange_x(0, None)
        w_bf = sb.tile([P, PASSES, N, 4], BF16, name="w_bf", align_bytes=64)
        nc.scalar.copy(out=w_bf[:].rearrange("p g (c i) j -> p g c j i", i=4), in_=w_raw[:].rearrange("p g j (c i) -> p g c j i", i=4))
        exchange_x(1, "w_raw")
        abz = [fetch_pair(f"abz{h}", mz_t, h) for h in range(2)]

        px = f32("px", [2, S])
        nc.vector.scalar_tensor_tensor(out=px[:, 0, :], in0=gy[:], scalar=-1.0, in1=mz_t[:], op0=ALU.mult, op1=ALU.mult)
        w_codes = sb.tile([P, PASSES * N], U32, name="w_codes", align_bytes=64)
        w_scales = sb.tile([P, PASSES * N], U8, name="w_scales", align_bytes=64)
        nc.vector.quantize_mx(out=w_codes[:].bitcast(FP8X4), scales=w_scales[:], in_=w_bf[:].rearrange("p g n j -> p (g n j)"))
        for h in range(2):
            nc.vector.tensor_copy(out=words[1][:, cols(h)], in_=word_win[1][:].indirect(offs_t[:, entries(h)]))

        x_bank = ps.tile([P, 4, BLK], F32, name="x_bank", tag="e_bank")
        for b in range(4):
            turn(x_bank[:, b, :], px[:, 0, b * BLK : (b + 1) * BLK], start=(b == 0), stop=False)

        y_bank = [ps.tile([P, 2, BLK], F32, name=f"y_bank{h}") for h in range(2)]
        y_t = f32("y_t", [4, BLK])
        for h in range(2):
            for g in range(PASSES):
                for b in range(2):
                    j0 = h * HALF + b * BLK
                    nc.tensor.matmul_mx(
                        out=y_bank[h][:, b, :],
                        lhsT=words[g][:, j0 : j0 + BLK].bitcast(FP8X4),
                        lhsT_scale=scales[4 * g : P, j0 : j0 + BLK],
                        rhs=w_codes[:, g * N : (g + 1) * N].bitcast(FP8X4),
                        rhs_scale=w_scales[:, g * N : (g + 1) * N],
                        start=(g == 0 and b == 0),
                        stop=(g == PASSES - 1 and b == 1),
                    )
            nc.scalar.copy(out=y_t[:, 2 * h : 2 * h + 2, :], in_=y_bank[h][:])
            for b in range(2):
                turn(ex_bank[h][:, b, :], y_t[:, 2 * h + b, :], start=False, stop=(b == 1))

        gz = f32("gz", [S])
        ngz = f32("ngz", [S])
        ngy = f32("ngy", [S], "win1")
        hx = f32("hx", [S])
        pyz = f32("pyz", [2, S])
        res = f32("res", [S])
        t_bank = [ps.tile([P, 2, BLK], F32, name=f"t_bank{c}", tag=("t_bank0", "y_bank0")[c]) for c in range(2)]

        for h in range(2):
            add(gz[:, cols(h)], abz[h][:, 0, :], abz[h][:, 1, :])
            mul(px[:, 1, cols(h)], gz[:, cols(h)], my_t[:, cols(h)])
            mul(ngz[:, cols(h)], nex[:, cols(h)], gz[:, cols(h)])
        for h in range(2):
            mul(ngy[:, cols(h)], nex[:, cols(h)], gy[:, cols(h)])
        for b in range(4):
            turn(x_bank[:, b, :], px[:, 1, b * BLK : (b + 1) * BLK], start=False, stop=(b == 3))
        for c in range(2):
            for b in range(2):
                turn(t_bank[c][:, b, :], (ngz, ngy)[c][:, b * BLK : (b + 1) * BLK], start=(b == 0), stop=False)
        sq_x = f32("sq_x", [4, BLK])
        for b in range(4):
            nc.scalar.activation(out=sq_x[:, b, :], in_=x_bank[:, b, :], func=ACT.Square, scale=e_col[:, b : b + 1])

        def product(h, c):
            mul(pyz[:, c, cols(h)], hx[:, cols(h)], (mz_t, my_t)[c][:, cols(h)])

        def finish(lo, hi, total):
            nc.scalar.activation(out=res[:, lo:hi], in_=total, func=ACT.Sqrt, bias=0.02)
            nc.sync.dma_start(out=out[:, lo:hi], in_=res[:, lo:hi])

        for h in range(2):
            nc.vector.scalar_tensor_tensor(out=hx[:, cols(h)], in0=mx_t[:, cols(h)], scalar=-0.3, in1=flat(ex_bank[h]), op0=ALU.mult, op1=ALU.add)
        sq_yz = f32("sq_yz", [2, 2, BLK])
        for c in range(2):
            product(0, c)
            for b in range(2):
                turn(t_bank[c][:, b, :], pyz[:, c, b * BLK : (b + 1) * BLK], start=False, stop=(b == 1))
            nc.scalar.activation(out=sq_yz[:, c, :, :], in_=t_bank[c][:], func=ACT.Square)
        out_bank = [ps.tile([P, 2, BLK], F32, name=f"out_bank{h}", tag=f"out{h}") for h in range(2)]
        for h in (1, 0):
            for b in range(2):
                turn(out_bank[h][:, b, :], sq_x[:, 2 * h + b, :], start=(b == 0), stop=(h == 1 and b == 1))
        for c in range(2):
            for b in range(2):
                turn(out_bank[0][:, b, :], sq_yz[:, c, b, :], start=False, stop=(c == 1 and b == 1))
        product(1, 0)
        product(1, 1)
        tyz = f32("tyz", [2, 2, BLK])
        sq1 = f32("sq1", [2, 2, BLK])
        part = f32("part", [2, 2, BLK])
        for b in range(2):
            j0 = HALF + b * BLK
            for c in range(2):
                add(tyz[:, b, c, :], pyz[:, c, j0 : j0 + BLK], (ngz, ngy)[c][:, j0 : j0 + BLK])
                nc.scalar.activation(out=sq1[:, b, c, :], in_=tyz[:, b, c, :], func=ACT.Square)
        finish(0, HALF, flat(out_bank[0]))
        for b in range(2):
            add(part[:, b, 0, :], out_bank[1][:, b, :], sq1[:, b, 0, :])
        for b in range(2):
            add(part[:, b, 1, :], part[:, b, 0, :], sq1[:, b, 1, :])
            finish(HALF + b * BLK, HALF + (b + 1) * BLK, part[:, b, 1, :])
